import numpy as np
import ml_dtypes


def mxq(x, axis, fmt="e4m3"):
    dtype, down = {"e4m3": (ml_dtypes.float8_e4m3fn, 7), "e5m2": (ml_dtypes.float8_e5m2, 14)}[fmt]
    v = np.moveaxis(np.asarray(x, np.float32).astype(ml_dtypes.bfloat16).astype(np.float64), axis, -1)
    blocks = v.reshape(v.shape[:-1] + (-1, 32))
    amax = np.abs(blocks).max(-1, keepdims=True)
    byte = np.maximum(np.where(amax > 0, np.frexp(amax)[1] - 1 + 127, 0) - down, 1)
    scale = np.exp2(byte - 127.0)
    codes = (blocks / scale).astype(np.float32).astype(dtype).astype(np.float64)
    return np.moveaxis((codes * scale).reshape(v.shape), -1, axis)


WIDE = False


def mx_kscale(k):
    if not WIDE:
        return np.ones(k)
    levels = np.array([10, -10, 5, -5, 0])
    if k % 512:
        return np.exp2(np.random.permutation(np.resize(levels, k // 32))).repeat(32)
    a = np.empty((k // 512, 16))
    for p in range(k // 512):
        a[p, :8] = np.random.permutation(np.resize(levels, 8))
        for g in range(8):
            far = levels[np.abs(levels - a[p, g]) >= 10]
            a[p, g + 8] = far[np.random.randint(len(far))]
    return np.exp2(a.ravel()).repeat(32)


def f64(x):
    return np.asarray(x).astype(np.float64)


def striped(idx):
    return np.tile(idx.reshape(-1, 16).T, (8, 1)).astype(np.uint16)


def unstriped(offs):
    return offs[:16].T.reshape(-1).astype(np.int64)


E2M1 = np.array([0.0, 0.5, 1.0, 1.5, 2.0, 3.0, 4.0, 6.0, -0.0, -0.5, -1.0, -1.5, -2.0, -3.0, -4.0, -6.0])


def pack_weight(w, fmt):
    k, n = w.shape
    w = f64(np.asarray(w, np.float32).astype(ml_dtypes.bfloat16)).reshape(k // 32, 32, n)
    amax = np.abs(w).max(1)
    if fmt == "e4m3":
        byte = np.frexp(amax)[1] - 1 + 127 - 7
    else:
        mant, ex = np.frexp(amax / 6.0)
        byte = np.where(mant > 0.5, ex, ex - 1) + 127
    byte = np.clip(np.where(amax > 0, byte, 1), 1, 254)
    scaled = (w * np.exp2(127.0 - byte)[:, None, :]).reshape(k, n).astype(np.float32)
    by_word = np.ascontiguousarray(scaled.reshape(k // 512, 128, 4, n).transpose(0, 1, 3, 2))
    if fmt == "e4m3":
        words = by_word.astype(ml_dtypes.float8_e4m3fn).view(np.uint8)
    else:
        c = by_word.astype(ml_dtypes.float4_e2m1fn).view(np.uint8) & 0xF
        words = (c[..., 0::2] | (c[..., 1::2] << 4)).reshape(k // 512, 128, 2 * n)
    return np.ascontiguousarray(words), np.ascontiguousarray(byte.astype(np.uint8).reshape(k // 512, 16, n))


def unpack_weight(words, scales, fmt):
    g, _, n = scales.shape
    words = np.ascontiguousarray(words).reshape(g, 128, n, -1)
    if fmt == "e4m3":
        vals = words.view(ml_dtypes.float8_e4m3fn).astype(np.float64)
    else:
        nib = np.empty((g, 128, n, 4), np.uint8)
        nib[..., 0::2] = words & 0xF
        nib[..., 1::2] = words >> 4
        vals = E2M1[nib]
    vals = vals * np.repeat(np.exp2(scales.astype(np.float64) - 127.0), 8, axis=1)[..., None]
    return vals.transpose(0, 1, 3, 2).reshape(g * 512, n)


def gelu(v):
    return 0.5 * v * (1.0 + np.tanh(np.sqrt(2.0 / np.pi) * (v + 0.044715 * v**3)))


K, T, S, H, T2, P, N = 1024, 2048, 1024, 1024, 2048, 1024, 512

def setup_inputs():
    n = np.random.standard_normal
    s = mx_kscale(K)[:, None]
    u = mx_kscale(H)[:, None]
    tab_words, tab_scales = pack_weight(n((K, T)) * s, "e4m3")
    w4_words, w4_scales = pack_weight(n((H, N)) / np.sqrt(H) / u, "e2m1")
    return {
        "tab_words": tab_words, "tab_scales": tab_scales,
        "w1": (n((K, H)) / np.sqrt(K) / s * u.T).astype(np.float32),
        "w4_words": w4_words, "w4_scales": w4_scales,
        "lift": (0.7 * n(H)).astype(np.float32),
        "page0": (n((H, T2)) * u).astype(np.float32),
        "base": (0.8 * n((H, P)) * u).astype(np.float32),
        "b2": (0.6 * n(N)).astype(np.float32),
        "offs": striped(np.random.permutation(T)[:S]),
        "offs2": striped(np.random.permutation(T2)[:S]),
        "offs3": striped(np.random.permutation(T2)[:P]),
    }

def reference(tab_words, tab_scales, w1, w4_words, w4_scales, lift, page0, base, b2, offs, offs2, offs3):
    v = unpack_weight(tab_words, tab_scales, "e4m3")[:, unstriped(offs)]
    w4 = unpack_weight(w4_words, w4_scales, "e2m1")
    h = mxq(f64(w1), 0, "e4m3").T @ v
    page = f64(page0).copy()
    l2 = unstriped(offs2)
    page[:, l2] = np.maximum(page[:, l2], h) + f64(lift)[:, None] * h
    x = page[:, unstriped(offs3)] + f64(base)
    y = w4.T @ mxq(x, 0, "e4m3")
    return np.abs(y + f64(b2)[:, None])

@@ -1,0 +1,248 @@
+from contextlib import ExitStack
+
+import concourse.mybir as mybir
+
+K, T, S, H, T2, J, N = 1024, 2048, 1024, 1024, 2048, 1024, 512
+FLOPS = 2 * K * H * S + 2 * H * N * J
+
+F32 = mybir.dt.float32
+BF16 = mybir.dt.bfloat16
+I32 = mybir.dt.int32
+U32 = mybir.dt.uint32
+U16 = mybir.dt.uint16
+U8 = mybir.dt.uint8
+E4M3 = mybir.dt.float8_e4m3fn_x4
+E2M1 = mybir.dt.float4_e2m1fn_x4
+ACT = mybir.ActivationFunctionType
+ALU = mybir.AluOpType
+
+P = 128
+PACK = 4
+PASS = P * PACK
+BANK = 512
+GROUP = 16
+SLICES = H // P
+CHUNKS = (256, 256, 256, 128, 128)
+
+
+def tile_list_substation_page_features_kernel(
+    tc, tab_words, tab_scales, w1, w4_words, w4_scales, lift, page0, base, b2, offs, offs2, offs3, out
+):
+    nc = tc.nc
+    with ExitStack() as ctx:
+        sb = ctx.enter_context(tc.tile_pool(name="sb", bufs=1))
+        ps = ctx.enter_context(tc.psum_pool(name="ps", bufs=1))
+
+        def tiles(name, count, shape, dtype):
+            return [sb.tile(shape, dtype, name=f"{name}{i}", align_bytes=64) for i in range(count)]
+
+        idx, idx2, idx3 = tiles("idx", 3, [P, S // GROUP], U16)
+        tab_w = tiles("tab_w", 2, [P, T], U32)
+        tab_s = sb.tile([P, T], U8, align_bytes=64)
+        v_w0 = sb.tile([P, S], U32, align_bytes=64)
+        v_w1 = tiles("v_w1", 2, [P, BANK], U32)
+        v_s = sb.tile([P, S], U8, align_bytes=64)
+        stage = tiles("stage", 4, [P, PACK * PASS], F32)
+        w1_bf = tiles("w1_bf", 4, [P, PACK * PASS], BF16)
+        w1_w = tiles("w1_w", 4, [P, PASS], U32)
+        w1_s = tiles("w1_s", 4, [P, PASS], U8)
+        page = tiles("page", SLICES, [P, T2], F32)
+        h_sb = tiles("h_sb", 2, [P, S], F32)
+        gap = tiles("gap", 2, [P, S], F32)
+        ring = tiles("ring", 3, [P, S], F32)
+        x_bf = tiles("x_bf", 3, [P, PACK * max(CHUNKS)], BF16)
+        x_w = tiles("x_w", 4, [P, max(CHUNKS)], U32)
+        x_s = tiles("x_s", 4, [P, max(CHUNKS)], U8)
+        w4_w = tiles("w4_w", 2, [P, 2 * N], U8)
+        w4_s = sb.tile([P, 2 * N], U8, align_bytes=64)
+        lift_sb = sb.tile([P, SLICES], F32, align_bytes=64)
+        lift1 = sb.tile([P, SLICES], F32, align_bytes=64)
+        b2_sb = sb.tile([P, N // P], F32, align_bytes=64)
+        res = tiles("res", len(CHUNKS), [P, (N // P) * max(CHUNKS)], F32)
+        banks = [ps.tile([P, BANK], F32, name=f"bank{i}") for i in range(8)]
+
+        def load_tab_words(a):
+            nc.sync.dma_start(tab_w[a][:].bitcast(I32), tab_words[a].rearrange("p t i -> p (t i)").bitcast(I32))
+
+        def load_w1(b, a):
+            nc.sync.dma_start(
+                stage[2 * b + a][:].rearrange("p (j c) -> p j c", j=PACK),
+                w1[a * PASS : (a + 1) * PASS, b * PASS : (b + 1) * PASS].rearrange("(p j) c -> p j c", j=PACK),
+            )
+
+        def load_page(k):
+            b, t = divmod(k, PACK)
+            nc.sync.dma_start(page[k][:], page0.rearrange("(b p t) c -> b t p c", p=P, t=PACK)[b, t])
+
+        def load_base(b, half):
+            nc.sync.dma_start(
+                stage[2 * half + b][:].rearrange("p (t j) -> p t j", t=PACK),
+                base[b * PASS : (b + 1) * PASS, half * BANK : (half + 1) * BANK].rearrange("(p t) j -> p t j", t=PACK),
+            )
+
+        def round_w1(copy, b, a):
+            copy(
+                w1_bf[2 * b + a][:].rearrange("p (t m j) -> p m t j", t=PACK, j=PACK),
+                stage[2 * b + a][:].rearrange("p (j m t) -> p m t j", j=PACK, t=PACK),
+            )
+
+        def quantize_w1(b, a):
+            i = 2 * b + a
+            nc.vector.quantize_mx(out=w1_w[i][:].bitcast(E4M3), scales=w1_s[i][:], in_=w1_bf[i][:])
+
+        def first_product(k, half):
+            b, t = divmod(k, PACK)
+            cols = slice(t * P, (t + 1) * P)
+            js = slice(half * BANK, (half + 1) * BANK)
+            for a in range(2):
+                words = v_w0[:, js] if a == 0 else v_w1[half][:]
+                nc.tensor.matmul_mx(
+                    out=banks[(2 * k + half) % 8][:],
+                    lhsT=w1_w[2 * b + a][:, cols].bitcast(E4M3),
+                    lhsT_scale=w1_s[2 * b + a][:, cols],
+                    rhs=words.bitcast(E4M3),
+                    rhs_scale=v_s[PACK * a : P, js],
+                    start=(a == 0),
+                    stop=(a == 1),
+                )
+
+        def make_h(k):
+            for half in range(2):
+                first_product(k, half)
+                nc.scalar.copy(h_sb[k % 2][:, half * BANK : (half + 1) * BANK], banks[(2 * k + half) % 8][:])
+
+        def fetch_old(k, pieces):
+            w = S // pieces
+            for i in range(pieces):
+                js = slice(i * w, (i + 1) * w)
+                nc.vector.tensor_tensor(
+                    gap[k % 2][:, js],
+                    page[k][:].indirect(idx2[:, i * w // GROUP : (i + 1) * w // GROUP]),
+                    h_sb[k % 2][:, js],
+                    ALU.subtract,
+                )
+
+        def put_new(k):
+            nc.scalar.activation(gap[k % 2][:], gap[k % 2][:], ACT.Relu)
+            for half in range(2):
+                nc.scalar.activation(
+                    ring[k % 3][:, half * BANK : (half + 1) * BANK],
+                    banks[(2 * k + half) % 8][:],
+                    ACT.Copy,
+                    scale=lift1[:, k : k + 1],
+                )
+            nc.vector.tensor_tensor(page[k][:].indirect(idx2[:]), gap[k % 2][:], ring[k % 3][:], ALU.add)
+
+        nc.vector.memset(tab_s[:].bitcast(I32), 0)
+        nc.gpsimd.memset(w4_s[:].bitcast(I32), 0)
+        nc.sync.dma_start(idx[:], offs)
+        load_tab_words(0)
+        for q in range(4):
+            nc.sync.dma_start(
+                tab_s[32 * q : 32 * q + 2 * PACK, :].bitcast(I32),
+                tab_scales[:, PACK * q : PACK * (q + 1), :].bitcast(I32),
+            )
+        load_w1(0, 0)
+        load_w1(0, 1)
+        load_tab_words(1)
+        nc.sync.dma_start(idx2[:], offs2)
+        load_page(0)
+        nc.sync.dma_start(
+            lift_sb[:].rearrange("p (b t) -> p b t", t=PACK), lift.rearrange("(b p t) -> p b t", p=P, t=PACK)
+        )
+        load_page(1)
+        load_w1(1, 0)
+        load_page(2)
+        load_w1(1, 1)
+        for k in range(3, SLICES):
+            load_page(k)
+
+        nc.vector.tensor_copy(v_w0[:], tab_w[0][:].indirect(idx[:]))
+        nc.vector.tensor_copy(v_s[:], tab_s[:].indirect(idx[:]))
+        round_w1(nc.scalar.copy, 0, 0)
+        round_w1(nc.vector.tensor_copy, 0, 1)
+        quantize_w1(0, 0)
+        quantize_w1(0, 1)
+        for half in range(2):
+            cols = slice(half * BANK // GROUP, (half + 1) * BANK // GROUP)
+            nc.vector.tensor_copy(v_w1[half][:], tab_w[1][:].indirect(idx[:, cols]))
+        nc.gpsimd.tensor_scalar(lift1[:], lift_sb[:], 1.0, 1.0, ALU.mult, ALU.add)
+
+        make_h(0)
+        fetch_old(0, 2)
+        for k in range(SLICES):
+            if k + 1 < SLICES:
+                make_h(k + 1)
+                fetch_old(k + 1, 1)
+            put_new(k)
+            if k < 2:
+                round_w1(nc.scalar.copy, 1, k)
+                quantize_w1(1, k)
+
+        nc.sync.dma_start(idx3[:], offs3)
+        for half in range(2):
+            for b in range(2):
+                load_base(b, half)
+        for a in range(2):
+            nc.sync.dma_start(w4_w[a][:].bitcast(I32), w4_words[a].bitcast(I32))
+        for q in range(4):
+            nc.sync.dma_start(
+                w4_s[32 * q : 32 * q + PACK, :].bitcast(I32).rearrange("r (a c) -> r a c", a=2),
+                w4_scales[:, PACK * q : PACK * (q + 1), :].bitcast(I32).rearrange("a r c -> r a c"),
+            )
+        with nc.allow_non_contiguous_dma(reason="one bias value for each partition and tile of n"):
+            nc.sync.dma_start(b2_sb[:], b2.rearrange("(u p) -> p u", p=P))
+
+        starts = [sum(CHUNKS[:c]) for c in range(len(CHUNKS))]
+        steps = [(c, b) for c in range(len(CHUNKS)) for b in range(2)]
+
+        def fetch_x(i):
+            c, b = steps[i]
+            j0, w = starts[c], CHUNKS[c]
+            half, off = divmod(j0, BANK)
+            x = ring[(SLICES + i) % 3]
+            for t in range(PACK):
+                nc.vector.tensor_tensor(
+                    x[:, t * w : (t + 1) * w],
+                    page[PACK * b + t][:].indirect(idx3[:, j0 // GROUP : (j0 + w) // GROUP]),
+                    stage[2 * half + b][:, t * BANK + off : t * BANK + off + w],
+                    ALU.add,
+                )
+            copy = nc.vector.tensor_copy if i == len(steps) - 1 else nc.scalar.copy
+            copy(
+                x_bf[i % 3][:, : PACK * w].rearrange("p (c i t) -> p c t i", i=4, t=PACK),
+                x[:, : PACK * w].rearrange("p (t c i) -> p c t i", t=PACK, i=4),
+            )
+
+        def second_product(i):
+            c, b = steps[i]
+            j0, w = starts[c], CHUNKS[c]
+            nc.vector.quantize_mx(
+                out=x_w[i % 4][:, :w].bitcast(E4M3), scales=x_s[i % 4][:, :w], in_=x_bf[i % 3][:, : PACK * w]
+            )
+            for u in range(N // P):
+                bank = banks[(4 * c + u) % 8]
+                nc.tensor.matmul_mx(
+                    out=bank[:, :w],
+                    lhsT=w4_w[b][:, 2 * u * P : 2 * (u + 1) * P].bitcast(E2M1),
+                    lhsT_scale=w4_s[:, b * N + u * P : b * N + (u + 1) * P],
+                    rhs=x_w[i % 4][:, :w].bitcast(E4M3),
+                    rhs_scale=x_s[i % 4][:, :w],
+                    start=(b == 0),
+                    stop=(b == 1),
+                )
+                if b == 1:
+                    nc.scalar.activation(
+                        res[c][:, u * w : (u + 1) * w], bank[:, :w], ACT.Abs, bias=b2_sb[:, u : u + 1]
+                    )
+            if b == 1:
+                nc.sync.dma_start(
+                    out[:, j0 : j0 + w].rearrange("(u p) j -> p u j", p=P),
+                    res[c][:, : (N // P) * w].rearrange("p (u j) -> p u j", j=w),
+                )
+
+        for i in range(len(steps) + 1):
+            if i < len(steps):
+                fetch_x(i)
+            if i > 0:
+                second_product(i - 1)

@@ -19,10 +19,14 @@ ALU = mybir.AluOpType
 P = 128
 PACK = 4
 PASS = P * PACK
+QUAD = 32
 BANK = 512
 GROUP = 16
+LINE = 4
 SLICES = H // P
+PIECE = 256
 CHUNKS = (256, 256, 256, 128, 128)
+VECTOR_ROUNDS = 2
 
 
 def tile_list_substation_page_features_kernel(
@@ -42,65 +46,92 @@ def tile_list_substation_page_features_kernel(
         v_w0 = sb.tile([P, S], U32, align_bytes=64)
         v_w1 = tiles("v_w1", 2, [P, BANK], U32)
         v_s = sb.tile([P, S], U8, align_bytes=64)
-        stage = tiles("stage", 4, [P, PACK * PASS], F32)
-        w1_bf = tiles("w1_bf", 4, [P, PACK * PASS], BF16)
-        w1_w = tiles("w1_w", 4, [P, PASS], U32)
-        w1_s = tiles("w1_s", 4, [P, PASS], U8)
+        stage_lo = tiles("stage_lo", PACK, [P, 2 * PACK * P], F32)
+        stage_hi = tiles("stage_hi", 2, [P, PACK * PASS], F32)
+        bf_lo = tiles("bf_lo", PACK, [P, 2 * PACK * P], BF16)
+        bf_hi = tiles("bf_hi", 2, [P, PACK * PASS], BF16)
+        w1_lo_w = tiles("w1_lo_w", PACK, [P, 2 * P], U32)
+        w1_lo_s = tiles("w1_lo_s", PACK, [P, 2 * P], U8)
+        w1_hi_w = tiles("w1_hi_w", 2, [P, PASS], U32)
+        w1_hi_s = tiles("w1_hi_s", 2, [P, PASS], U8)
         page = tiles("page", SLICES, [P, T2], F32)
         h_sb = tiles("h_sb", 2, [P, S], F32)
-        gap = tiles("gap", 2, [P, S], F32)
-        ring = tiles("ring", 3, [P, S], F32)
-        x_bf = tiles("x_bf", 3, [P, PACK * max(CHUNKS)], BF16)
-        x_w = tiles("x_w", 4, [P, max(CHUNKS)], U32)
-        x_s = tiles("x_s", 4, [P, max(CHUNKS)], U8)
+        gap = tiles("gap", 3, [P, S], F32)
+        ring = tiles("ring", 2, [P, S], F32)
+        x_rows = tiles("x_rows", 2, [P, J], F32)
+        x_dealt = sb.tile([P, PACK * J], F32, align_bytes=64)
+        x_lo_s = sb.tile([P, J], U8, align_bytes=64)
+        x_bf = tiles("x_bf", 2, [P, PACK * max(CHUNKS)], BF16)
+        x_hi_w = tiles("x_hi_w", 2, [P, max(CHUNKS)], U32)
+        x_hi_s = tiles("x_hi_s", 2, [P, max(CHUNKS)], U8)
         w4_w = tiles("w4_w", 2, [P, 2 * N], U8)
         w4_s = sb.tile([P, 2 * N], U8, align_bytes=64)
-        lift_sb = sb.tile([P, SLICES], F32, align_bytes=64)
-        lift1 = sb.tile([P, SLICES], F32, align_bytes=64)
+        lift_sb = tiles("lift_sb", SLICES, [P, 1], F32)
+        lift1 = tiles("lift1", SLICES, [P, 1], F32)
         b2_sb = sb.tile([P, N // P], F32, align_bytes=64)
-        res = tiles("res", len(CHUNKS), [P, (N // P) * max(CHUNKS)], F32)
+        res = [sb.tile([P, (N // P) * w], F32, name=f"res{c}", align_bytes=64) for c, w in enumerate(CHUNKS)]
         banks = [ps.tile([P, BANK], F32, name=f"bank{i}") for i in range(8)]
 
-        def load_tab_words(a):
-            nc.sync.dma_start(tab_w[a][:].bitcast(I32), tab_words[a].rearrange("p t i -> p (t i)").bitcast(I32))
+        h_of = [stage_lo[k + 1] if k + 1 < PACK else h_sb[k % 2] for k in range(SLICES)]
 
-        def load_w1(b, a):
-            nc.sync.dma_start(
-                stage[2 * b + a][:].rearrange("p (j c) -> p j c", j=PACK),
-                w1[a * PASS : (a + 1) * PASS, b * PASS : (b + 1) * PASS].rearrange("(p j) c -> p j c", j=PACK),
+        def rows_of(dram, k):
+            if k < PACK:
+                return dram[k * P : (k + 1) * P, :]
+            return dram[PASS:, :].rearrange("(p t) c -> t p c", t=PACK)[k - PACK]
+
+        def load_tab_words(a, pieces):
+            words = tab_words[a].rearrange("p t i -> p (t i)").bitcast(I32)
+            for i in range(pieces):
+                cols = slice(i * T // pieces, (i + 1) * T // pieces)
+                nc.sync.dma_start(tab_w[a][:, cols].bitcast(I32), words[:, cols])
+
+        def load_w1_lo(u):
+            for a in range(2):
+                nc.sync.dma_start(
+                    stage_lo[u][:, a * PASS : (a + 1) * PASS].rearrange("p (j c) -> p j c", j=PACK),
+                    w1[a * PASS : (a + 1) * PASS, u * P : (u + 1) * P].rearrange("(p j) c -> p j c", j=PACK),
+                )
+
+        def load_w1_hi():
+            for a in range(2):
+                nc.sync.dma_start(
+                    stage_hi[a][:].rearrange("p (j c) -> p j c", j=PACK),
+                    w1[a * PASS : (a + 1) * PASS, PASS:].rearrange("(p j) c -> p j c", j=PACK),
+                )
+
+        def load_lift(k):
+            with nc.allow_non_contiguous_dma(reason="one value of lift for each partition"):
+                nc.sync.dma_start(lift_sb[k][:], rows_of(lift.rearrange("(r o) -> r o", o=1), k))
+
+        def quantize_w1_lo(u):
+            for a in range(2):
+                cols = slice(a * PASS, (a + 1) * PASS)
+                nc.scalar.copy(
+                    bf_lo[u][:, cols].rearrange("p (c i j) -> p c j i", i=LINE, j=PACK),
+                    stage_lo[u][:, cols].rearrange("p (j c i) -> p c j i", j=PACK, i=LINE),
+                )
+            nc.vector.quantize_mx(out=w1_lo_w[u][:].bitcast(E4M3), scales=w1_lo_s[u][:], in_=bf_lo[u][:])
+
+        def quantize_w1_hi(a):
+            nc.scalar.copy(
+                bf_hi[a][:].rearrange("p (t m j) -> p m t j", t=PACK, j=PACK),
+                stage_hi[a][:].rearrange("p (j m t) -> p m t j", j=PACK, t=PACK),
             )
-
-        def load_page(k):
-            b, t = divmod(k, PACK)
-            nc.sync.dma_start(page[k][:], page0.rearrange("(b p t) c -> b t p c", p=P, t=PACK)[b, t])
-
-        def load_base(b, half):
-            nc.sync.dma_start(
-                stage[2 * half + b][:].rearrange("p (t j) -> p t j", t=PACK),
-                base[b * PASS : (b + 1) * PASS, half * BANK : (half + 1) * BANK].rearrange("(p t) j -> p t j", t=PACK),
-            )
-
-        def round_w1(copy, b, a):
-            copy(
-                w1_bf[2 * b + a][:].rearrange("p (t m j) -> p m t j", t=PACK, j=PACK),
-                stage[2 * b + a][:].rearrange("p (j m t) -> p m t j", j=PACK, t=PACK),
-            )
-
-        def quantize_w1(b, a):
-            i = 2 * b + a
-            nc.vector.quantize_mx(out=w1_w[i][:].bitcast(E4M3), scales=w1_s[i][:], in_=w1_bf[i][:])
+            nc.vector.quantize_mx(out=w1_hi_w[a][:].bitcast(E4M3), scales=w1_hi_s[a][:], in_=bf_hi[a][:])
 
         def first_product(k, half):
-            b, t = divmod(k, PACK)
-            cols = slice(t * P, (t + 1) * P)
             js = slice(half * BANK, (half + 1) * BANK)
             for a in range(2):
-                words = v_w0[:, js] if a == 0 else v_w1[half][:]
+                if k < PACK:
+                    w_words, w_scales, cols = w1_lo_w[k], w1_lo_s[k], slice(a * P, (a + 1) * P)
+                else:
+                    w_words, w_scales, cols = w1_hi_w[a], w1_hi_s[a], slice((k - PACK) * P, (k - PACK + 1) * P)
+                v_words = v_w0[:, js] if a == 0 else v_w1[half][:]
                 nc.tensor.matmul_mx(
                     out=banks[(2 * k + half) % 8][:],
-                    lhsT=w1_w[2 * b + a][:, cols].bitcast(E4M3),
-                    lhsT_scale=w1_s[2 * b + a][:, cols],
-                    rhs=words.bitcast(E4M3),
+                    lhsT=w_words[:, cols].bitcast(E4M3),
+                    lhsT_scale=w_scales[:, cols],
+                    rhs=v_words.bitcast(E4M3),
                     rhs_scale=v_s[PACK * a : P, js],
                     start=(a == 0),
                     stop=(a == 1),
@@ -109,140 +140,170 @@ def tile_list_substation_page_features_kernel(
         def make_h(k):
             for half in range(2):
                 first_product(k, half)
-                nc.scalar.copy(h_sb[k % 2][:, half * BANK : (half + 1) * BANK], banks[(2 * k + half) % 8][:])
+                nc.scalar.copy(h_of[k][:, half * BANK : (half + 1) * BANK], banks[(2 * k + half) % 8][:])
 
         def fetch_old(k, pieces):
             w = S // pieces
             for i in range(pieces):
                 js = slice(i * w, (i + 1) * w)
                 nc.vector.tensor_tensor(
-                    gap[k % 2][:, js],
+                    gap[k % 3][:, js],
                     page[k][:].indirect(idx2[:, i * w // GROUP : (i + 1) * w // GROUP]),
-                    h_sb[k % 2][:, js],
+                    h_of[k][:, js],
                     ALU.subtract,
                 )
 
         def put_new(k):
-            nc.scalar.activation(gap[k % 2][:], gap[k % 2][:], ACT.Relu)
+            nc.scalar.activation(lift1[k][:], lift_sb[k][:], ACT.Copy, bias=1.0)
             for half in range(2):
                 nc.scalar.activation(
-                    ring[k % 3][:, half * BANK : (half + 1) * BANK],
+                    ring[k % 2][:, half * BANK : (half + 1) * BANK],
                     banks[(2 * k + half) % 8][:],
                     ACT.Copy,
-                    scale=lift1[:, k : k + 1],
+                    scale=lift1[k][:],
                 )
-            nc.vector.tensor_tensor(page[k][:].indirect(idx2[:]), gap[k % 2][:], ring[k % 3][:], ALU.add)
+            nc.scalar.activation(gap[k % 3][:], gap[k % 3][:], ACT.Relu)
+            nc.vector.tensor_tensor(page[k][:].indirect(idx2[:]), gap[k % 3][:], ring[k % 2][:], ALU.add)
 
-        nc.vector.memset(tab_s[:].bitcast(I32), 0)
-        nc.gpsimd.memset(w4_s[:].bitcast(I32), 0)
+        def fetch_x_lo(u):
+            nc.vector.tensor_tensor(x_rows[u % 2][:], page[u][:].indirect(idx3[:]), stage_lo[u][:], ALU.add)
+            nc.gpsimd.dma_start(x_dealt[QUAD * u : QUAD * (u + 1), :], x_rows[u % 2][:])
+
+        def round_x(copy, dst, src):
+            copy(
+                dst.rearrange("p (c i t) -> p c t i", i=LINE, t=PACK),
+                src.rearrange("p t (c i) -> p c t i", i=LINE),
+            )
+
+        nc.gpsimd.memset(tab_s[:].bitcast(I32), 0)
+        nc.vector.memset(w4_s[:].bitcast(I32), 0)
         nc.sync.dma_start(idx[:], offs)
-        load_tab_words(0)
-        for q in range(4):
+        load_tab_words(0, 2)
+        nc.sync.dma_start(idx2[:], offs2)
+        nc.sync.dma_start(idx3[:], offs3)
+        for q in range(P // QUAD):
             nc.sync.dma_start(
-                tab_s[32 * q : 32 * q + 2 * PACK, :].bitcast(I32),
+                tab_s[QUAD * q : QUAD * q + 2 * PACK, :].bitcast(I32),
                 tab_scales[:, PACK * q : PACK * (q + 1), :].bitcast(I32),
             )
-        load_w1(0, 0)
-        load_w1(0, 1)
-        load_tab_words(1)
-        nc.sync.dma_start(idx2[:], offs2)
-        load_page(0)
-        nc.sync.dma_start(
-            lift_sb[:].rearrange("p (b t) -> p b t", t=PACK), lift.rearrange("(b p t) -> p b t", p=P, t=PACK)
-        )
-        load_page(1)
-        load_w1(1, 0)
-        load_page(2)
-        load_w1(1, 1)
-        for k in range(3, SLICES):
-            load_page(k)
+        load_w1_lo(0)
+        load_tab_words(1, 1)
+        load_w1_lo(1)
+        nc.sync.dma_start(page[0][:], rows_of(page0, 0))
 
         nc.vector.tensor_copy(v_w0[:], tab_w[0][:].indirect(idx[:]))
         nc.vector.tensor_copy(v_s[:], tab_s[:].indirect(idx[:]))
-        round_w1(nc.scalar.copy, 0, 0)
-        round_w1(nc.vector.tensor_copy, 0, 1)
-        quantize_w1(0, 0)
-        quantize_w1(0, 1)
+        quantize_w1_lo(0)
         for half in range(2):
             cols = slice(half * BANK // GROUP, (half + 1) * BANK // GROUP)
             nc.vector.tensor_copy(v_w1[half][:], tab_w[1][:].indirect(idx[:, cols]))
-        nc.gpsimd.tensor_scalar(lift1[:], lift_sb[:], 1.0, 1.0, ALU.mult, ALU.add)
-
+        quantize_w1_lo(1)
         make_h(0)
         fetch_old(0, 2)
+
         for k in range(SLICES):
+            if k + 2 < PACK:
+                load_w1_lo(k + 2)
+                quantize_w1_lo(k + 2)
+            if k + 2 == PACK:
+                load_w1_hi()
+                for a in range(2):
+                    quantize_w1_hi(a)
             if k + 1 < SLICES:
+                nc.sync.dma_start(page[k + 1][:], rows_of(page0, k + 1))
                 make_h(k + 1)
                 fetch_old(k + 1, 1)
+            load_lift(k)
             put_new(k)
-            if k < 2:
-                round_w1(nc.scalar.copy, 1, k)
-                quantize_w1(1, k)
+            if 1 <= k <= PACK:
+                nc.sync.dma_start(stage_lo[k - 1][:], rows_of(base, k - 1))
+                fetch_x_lo(k - 1)
 
-        nc.sync.dma_start(idx3[:], offs3)
         for half in range(2):
-            for b in range(2):
-                load_base(b, half)
+            nc.sync.dma_start(
+                stage_hi[half][:].rearrange("p (t j) -> p t j", t=PACK),
+                base[PASS:, half * BANK : (half + 1) * BANK].rearrange("(p t) j -> p t j", t=PACK),
+            )
         for a in range(2):
             nc.sync.dma_start(w4_w[a][:].bitcast(I32), w4_words[a].bitcast(I32))
-        for q in range(4):
+        for q in range(P // QUAD):
             nc.sync.dma_start(
-                w4_s[32 * q : 32 * q + PACK, :].bitcast(I32).rearrange("r (a c) -> r a c", a=2),
+                w4_s[QUAD * q : QUAD * q + PACK, :].bitcast(I32).rearrange("r (a c) -> r a c", a=2),
                 w4_scales[:, PACK * q : PACK * (q + 1), :].bitcast(I32).rearrange("a r c -> r a c"),
             )
         with nc.allow_non_contiguous_dma(reason="one bias value for each partition and tile of n"):
             nc.sync.dma_start(b2_sb[:], b2.rearrange("(u p) -> p u", p=P))
 
-        starts = [sum(CHUNKS[:c]) for c in range(len(CHUNKS))]
-        steps = [(c, b) for c in range(len(CHUNKS)) for b in range(2)]
+        x_lo_bf = [
+            sb.tile([P, 2 * PACK * PIECE], BF16, name=f"x_lo_bf{i}", tag=tag, align_bytes=64)
+            for i, tag in enumerate((f"gap{(SLICES - 3) % 3}", f"h_sb{(SLICES - 1) % 2}"))
+        ]
+        x_lo_pieces = [
+            x_lo_bf[i // 2][:, (i % 2) * PACK * PIECE : (i % 2 + 1) * PACK * PIECE] for i in range(J // PIECE)
+        ]
+        for i in range(J // PIECE):
+            round_x(
+                nc.scalar.copy,
+                x_lo_pieces[i],
+                x_dealt[:].rearrange("p (t j) -> p t j", t=PACK)[:, :, i * PIECE : (i + 1) * PIECE],
+            )
 
-        def fetch_x(i):
-            c, b = steps[i]
+        x_lo_w = sb.tile([P, J], U32, tag=f"gap{(SLICES - 1) % 3}", align_bytes=64)
+        starts = [sum(CHUNKS[:c]) for c in range(len(CHUNKS))]
+
+        def fetch_x_hi(c):
             j0, w = starts[c], CHUNKS[c]
             half, off = divmod(j0, BANK)
-            x = ring[(SLICES + i) % 3]
             for t in range(PACK):
                 nc.vector.tensor_tensor(
-                    x[:, t * w : (t + 1) * w],
-                    page[PACK * b + t][:].indirect(idx3[:, j0 // GROUP : (j0 + w) // GROUP]),
-                    stage[2 * half + b][:, t * BANK + off : t * BANK + off + w],
+                    ring[c % 2][:, t * w : (t + 1) * w],
+                    page[PACK + t][:].indirect(idx3[:, j0 // GROUP : (j0 + w) // GROUP]),
+                    stage_hi[half][:, t * BANK + off : t * BANK + off + w],
                     ALU.add,
                 )
-            copy = nc.vector.tensor_copy if i == len(steps) - 1 else nc.scalar.copy
-            copy(
-                x_bf[i % 3][:, : PACK * w].rearrange("p (c i t) -> p c t i", i=4, t=PACK),
-                x[:, : PACK * w].rearrange("p (t c i) -> p c t i", t=PACK, i=4),
+            if j0 % PIECE == 0:
+                js = slice(j0, j0 + PIECE)
+                nc.vector.quantize_mx(out=x_lo_w[:, js].bitcast(E4M3), scales=x_lo_s[:, js], in_=x_lo_pieces[j0 // PIECE])
+            round_x(
+                nc.vector.tensor_copy if c >= len(CHUNKS) - VECTOR_ROUNDS else nc.scalar.copy,
+                x_bf[c % 2][:, : PACK * w],
+                ring[c % 2][:, : PACK * w].rearrange("p (t j) -> p t j", t=PACK),
             )
 
-        def second_product(i):
-            c, b = steps[i]
+        def second_product(c):
             j0, w = starts[c], CHUNKS[c]
             nc.vector.quantize_mx(
-                out=x_w[i % 4][:, :w].bitcast(E4M3), scales=x_s[i % 4][:, :w], in_=x_bf[i % 3][:, : PACK * w]
+                out=x_hi_w[c % 2][:, :w].bitcast(E4M3), scales=x_hi_s[c % 2][:, :w], in_=x_bf[c % 2][:, : PACK * w]
             )
-            for u in range(N // P):
-                bank = banks[(4 * c + u) % 8]
-                nc.tensor.matmul_mx(
-                    out=bank[:, :w],
-                    lhsT=w4_w[b][:, 2 * u * P : 2 * (u + 1) * P].bitcast(E2M1),
-                    lhsT_scale=w4_s[:, b * N + u * P : b * N + (u + 1) * P],
-                    rhs=x_w[i % 4][:, :w].bitcast(E4M3),
-                    rhs_scale=x_s[i % 4][:, :w],
-                    start=(b == 0),
-                    stop=(b == 1),
-                )
-                if b == 1:
-                    nc.scalar.activation(
-                        res[c][:, u * w : (u + 1) * w], bank[:, :w], ACT.Abs, bias=b2_sb[:, u : u + 1]
+            operands = (
+                (x_lo_w[:, j0 : j0 + w], x_lo_s[:, j0 : j0 + w]),
+                (x_hi_w[c % 2][:, :w], x_hi_s[c % 2][:, :w]),
+            )
+            for b, (x_words, x_scales) in enumerate(operands):
+                for u in range(N // P):
+                    nc.tensor.matmul_mx(
+                        out=banks[(PACK * c + u) % 8][:, :w],
+                        lhsT=w4_w[b][:, 2 * u * P : 2 * (u + 1) * P].bitcast(E2M1),
+                        lhsT_scale=w4_s[:, b * N + u * P : b * N + (u + 1) * P],
+                        rhs=x_words.bitcast(E4M3),
+                        rhs_scale=x_scales,
+                        start=(b == 0),
+                        stop=(b == 1),
                     )
-            if b == 1:
-                nc.sync.dma_start(
-                    out[:, j0 : j0 + w].rearrange("(u p) j -> p u j", p=P),
-                    res[c][:, : (N // P) * w].rearrange("p (u j) -> p u j", j=w),
+            for u in range(N // P):
+                nc.scalar.activation(
+                    res[c][:, u * w : (u + 1) * w], banks[(PACK * c + u) % 8][:, :w], ACT.Abs, bias=b2_sb[:, u : u + 1]
                 )
+            dst = out[:, j0 : j0 + w].rearrange("(u p) j -> p u j", p=P)
+            src = res[c][:].rearrange("p (u j) -> p u j", j=w)
+            if c + 1 < len(CHUNKS):
+                nc.sync.dma_start(dst, src)
+            else:
+                nc.sync.dma_start(dst[:, :2], src[:, :2])
+                nc.scalar.dma_start(dst[:, 2:], src[:, 2:])
 
-        for i in range(len(steps) + 1):
-            if i < len(steps):
-                fetch_x(i)
-            if i > 0:
-                second_product(i - 1)
+        for c in range(len(CHUNKS) + 1):
+            if c < len(CHUNKS):
+                fetch_x_hi(c)
+            if c > 0:
+                second_product(c - 1)

@@ -55,11 +55,11 @@ def tile_list_substation_page_features_kernel(
         w1_hi_w = tiles("w1_hi_w", 2, [P, PASS], U32)
         w1_hi_s = tiles("w1_hi_s", 2, [P, PASS], U8)
         page = tiles("page", SLICES, [P, T2], F32)
-        h_sb = tiles("h_sb", 2, [P, S], F32)
+        h_sb = tiles("h_sb", 3, [P, S], F32)
         gap = tiles("gap", 3, [P, S], F32)
         ring = tiles("ring", 2, [P, S], F32)
-        x_rows = tiles("x_rows", 2, [P, J], F32)
         x_dealt = sb.tile([P, PACK * J], F32, align_bytes=64)
+        x_lo_w = sb.tile([P, J], U32, align_bytes=64)
         x_lo_s = sb.tile([P, J], U8, align_bytes=64)
         x_bf = tiles("x_bf", 2, [P, PACK * max(CHUNKS)], BF16)
         x_hi_w = tiles("x_hi_w", 2, [P, max(CHUNKS)], U32)
@@ -72,7 +72,7 @@ def tile_list_substation_page_features_kernel(
         res = [sb.tile([P, (N // P) * w], F32, name=f"res{c}", align_bytes=64) for c, w in enumerate(CHUNKS)]
         banks = [ps.tile([P, BANK], F32, name=f"bank{i}") for i in range(8)]
 
-        h_of = [stage_lo[k + 1] if k + 1 < PACK else h_sb[k % 2] for k in range(SLICES)]
+        scaled = stage_lo[1:] + [stage_hi[1]] + [ring[k % 2] for k in range(PACK, SLICES)]
 
         def rows_of(dram, k):
             if k < PACK:
@@ -140,7 +140,7 @@ def tile_list_substation_page_features_kernel(
         def make_h(k):
             for half in range(2):
                 first_product(k, half)
-                nc.scalar.copy(h_of[k][:, half * BANK : (half + 1) * BANK], banks[(2 * k + half) % 8][:])
+                nc.scalar.copy(h_sb[k % 3][:, half * BANK : (half + 1) * BANK], banks[(2 * k + half) % 8][:])
 
         def fetch_old(k, pieces):
             w = S // pieces
@@ -149,25 +149,29 @@ def tile_list_substation_page_features_kernel(
                 nc.vector.tensor_tensor(
                     gap[k % 3][:, js],
                     page[k][:].indirect(idx2[:, i * w // GROUP : (i + 1) * w // GROUP]),
-                    h_of[k][:, js],
+                    h_sb[k % 3][:, js],
                     ALU.subtract,
                 )
+
+        def scale_h(k, half, dst):
+            nc.scalar.activation(dst, banks[(2 * k + half) % 8][:], ACT.Copy, scale=lift1[k][:])
+
+        def scatter(k, js, addend):
+            nc.scalar.activation(gap[k % 3][:, js], gap[k % 3][:, js], ACT.Relu)
+            offsets = idx2[:, js.start // GROUP : js.stop // GROUP]
+            nc.vector.tensor_tensor(page[k][:].indirect(offsets), gap[k % 3][:, js], addend, ALU.add)
 
         def put_new(k):
             nc.scalar.activation(lift1[k][:], lift_sb[k][:], ACT.Copy, bias=1.0)
             for half in range(2):
-                nc.scalar.activation(
-                    ring[k % 2][:, half * BANK : (half + 1) * BANK],
-                    banks[(2 * k + half) % 8][:],
-                    ACT.Copy,
-                    scale=lift1[k][:],
-                )
-            nc.scalar.activation(gap[k % 3][:], gap[k % 3][:], ACT.Relu)
-            nc.vector.tensor_tensor(page[k][:].indirect(idx2[:]), gap[k % 3][:], ring[k % 2][:], ALU.add)
+                scale_h(k, half, scaled[k][:, half * BANK : (half + 1) * BANK])
+            scatter(k, slice(0, S), scaled[k][:, :S])
 
         def fetch_x_lo(u):
-            nc.vector.tensor_tensor(x_rows[u % 2][:], page[u][:].indirect(idx3[:]), stage_lo[u][:], ALU.add)
-            nc.gpsimd.dma_start(x_dealt[QUAD * u : QUAD * (u + 1), :], x_rows[u % 2][:])
+            nc.vector.tensor_tensor(h_sb[(u + 1) % 3][:], page[u][:].indirect(idx3[:]), stage_lo[u][:], ALU.add)
+
+        def deal_x_lo(u):
+            nc.scalar.dma_start(x_dealt[QUAD * u : QUAD * (u + 1), :], h_sb[(u + 1) % 3][:])
 
         def round_x(copy, dst, src):
             copy(
@@ -178,18 +182,17 @@ def tile_list_substation_page_features_kernel(
         nc.gpsimd.memset(tab_s[:].bitcast(I32), 0)
         nc.vector.memset(w4_s[:].bitcast(I32), 0)
         nc.sync.dma_start(idx[:], offs)
-        load_tab_words(0, 2)
+        load_tab_words(0, 4)
         nc.sync.dma_start(idx2[:], offs2)
-        nc.sync.dma_start(idx3[:], offs3)
+        load_w1_lo(0)
         for q in range(P // QUAD):
             nc.sync.dma_start(
                 tab_s[QUAD * q : QUAD * q + 2 * PACK, :].bitcast(I32),
                 tab_scales[:, PACK * q : PACK * (q + 1), :].bitcast(I32),
             )
-        load_w1_lo(0)
         load_tab_words(1, 1)
-        load_w1_lo(1)
         nc.sync.dma_start(page[0][:], rows_of(page0, 0))
+        load_lift(0)
 
         nc.vector.tensor_copy(v_w0[:], tab_w[0][:].indirect(idx[:]))
         nc.vector.tensor_copy(v_s[:], tab_s[:].indirect(idx[:]))
@@ -197,27 +200,46 @@ def tile_list_substation_page_features_kernel(
         for half in range(2):
             cols = slice(half * BANK // GROUP, (half + 1) * BANK // GROUP)
             nc.vector.tensor_copy(v_w1[half][:], tab_w[1][:].indirect(idx[:, cols]))
-        quantize_w1_lo(1)
         make_h(0)
         fetch_old(0, 2)
+        nc.scalar.activation(lift1[0][:], lift_sb[0][:], ACT.Copy, bias=1.0)
+        scale_h(0, 0, ring[0][:, :BANK])
+        scatter(0, slice(0, BANK), ring[0][:, :BANK])
+        load_w1_lo(1)
+        quantize_w1_lo(1)
+        scale_h(0, 1, stage_lo[1][:, :BANK])
+        scatter(0, slice(BANK, S), stage_lo[1][:, :BANK])
 
-        for k in range(SLICES):
-            if k + 2 < PACK:
-                load_w1_lo(k + 2)
-                quantize_w1_lo(k + 2)
-            if k + 2 == PACK:
+        nc.sync.dma_start(idx3[:], offs3)
+
+        def fetch_slice(k):
+            nc.sync.dma_start(page[k][:], rows_of(page0, k))
+            make_h(k)
+            fetch_old(k, 1)
+
+        for k in range(1, SLICES):
+            if k < PACK:
+                load_lift(k)
+            if k + 1 < PACK:
+                load_w1_lo(k + 1)
+            if k + 1 == PACK:
                 load_w1_hi()
+            if k <= PACK:
+                nc.sync.dma_start(stage_lo[k - 1][:], rows_of(base, k - 1))
+                fetch_slice(k)
+                fetch_x_lo(k - 1)
+            if k + 1 < PACK:
+                quantize_w1_lo(k + 1)
+            if k + 1 == PACK:
                 for a in range(2):
                     quantize_w1_hi(a)
-            if k + 1 < SLICES:
-                nc.sync.dma_start(page[k + 1][:], rows_of(page0, k + 1))
-                make_h(k + 1)
-                fetch_old(k + 1, 1)
-            load_lift(k)
+            if PACK <= k < SLICES - 1:
+                fetch_slice(k + 1)
+            if k >= PACK:
+                load_lift(k)
             put_new(k)
-            if 1 <= k <= PACK:
-                nc.sync.dma_start(stage_lo[k - 1][:], rows_of(base, k - 1))
-                fetch_x_lo(k - 1)
+            if k <= PACK:
+                deal_x_lo(k - 1)
 
         for half in range(2):
             nc.sync.dma_start(
@@ -236,7 +258,7 @@ def tile_list_substation_page_features_kernel(
 
         x_lo_bf = [
             sb.tile([P, 2 * PACK * PIECE], BF16, name=f"x_lo_bf{i}", tag=tag, align_bytes=64)
-            for i, tag in enumerate((f"gap{(SLICES - 3) % 3}", f"h_sb{(SLICES - 1) % 2}"))
+            for i, tag in enumerate((f"h_sb{(SLICES - 1) % 3}", f"ring{(SLICES - 2) % 2}"))
         ]
         x_lo_pieces = [
             x_lo_bf[i // 2][:, (i % 2) * PACK * PIECE : (i % 2 + 1) * PACK * PIECE] for i in range(J // PIECE)
@@ -248,7 +270,7 @@ def tile_list_substation_page_features_kernel(
                 x_dealt[:].rearrange("p (t j) -> p t j", t=PACK)[:, :, i * PIECE : (i + 1) * PIECE],
             )
 
-        x_lo_w = sb.tile([P, J], U32, tag=f"gap{(SLICES - 1) % 3}", align_bytes=64)
+        x_hi = (ring[(SLICES - 1) % 2], gap[(SLICES - 1) % 3])
         starts = [sum(CHUNKS[:c]) for c in range(len(CHUNKS))]
 
         def fetch_x_hi(c):
@@ -256,7 +278,7 @@ def tile_list_substation_page_features_kernel(
             half, off = divmod(j0, BANK)
             for t in range(PACK):
                 nc.vector.tensor_tensor(
-                    ring[c % 2][:, t * w : (t + 1) * w],
+                    x_hi[c % 2][:, t * w : (t + 1) * w],
                     page[PACK + t][:].indirect(idx3[:, j0 // GROUP : (j0 + w) // GROUP]),
                     stage_hi[half][:, t * BANK + off : t * BANK + off + w],
                     ALU.add,
@@ -267,7 +289,7 @@ def tile_list_substation_page_features_kernel(
             round_x(
                 nc.vector.tensor_copy if c >= len(CHUNKS) - VECTOR_ROUNDS else nc.scalar.copy,
                 x_bf[c % 2][:, : PACK * w],
-                ring[c % 2][:, : PACK * w].rearrange("p (t j) -> p t j", t=PACK),
+                x_hi[c % 2][:, : PACK * w].rearrange("p (t j) -> p t j", t=PACK),
             )
 
         def second_product(c):

@@ -19,14 +19,22 @@ ALU = mybir.AluOpType
 P = 128
 PACK = 4
 PASS = P * PACK
+PASSES = 2
 QUAD = 32
+SCALE_ROWS = 4
 BANK = 512
+BANKS = 8
 GROUP = 16
-LINE = 4
+RUN = 4
 SLICES = H // P
+LOW = PASS // P
+N_TILES = N // P
 PIECE = 256
 CHUNKS = (256, 256, 256, 128, 128)
 VECTOR_ROUNDS = 2
+FIRST_LOADS = 4
+GAPS = 3
+RINGS = 2
 
 
 def tile_list_substation_page_features_kernel(
@@ -41,236 +49,227 @@ def tile_list_substation_page_features_kernel(
             return [sb.tile(shape, dtype, name=f"{name}{i}", align_bytes=64) for i in range(count)]
 
         idx, idx2, idx3 = tiles("idx", 3, [P, S // GROUP], U16)
-        tab_w = tiles("tab_w", 2, [P, T], U32)
+        tab_w = tiles("tab_w", PASSES, [P, T], U32)
         tab_s = sb.tile([P, T], U8, align_bytes=64)
         v_w0 = sb.tile([P, S], U32, align_bytes=64)
-        v_w1 = tiles("v_w1", 2, [P, BANK], U32)
+        v_w1 = tiles("v_w1", S // BANK, [P, BANK], U32)
         v_s = sb.tile([P, S], U8, align_bytes=64)
-        stage_lo = tiles("stage_lo", PACK, [P, 2 * PACK * P], F32)
-        stage_hi = tiles("stage_hi", 2, [P, PACK * PASS], F32)
-        bf_lo = tiles("bf_lo", PACK, [P, 2 * PACK * P], BF16)
-        bf_hi = tiles("bf_hi", 2, [P, PACK * PASS], BF16)
-        w1_lo_w = tiles("w1_lo_w", PACK, [P, 2 * P], U32)
-        w1_lo_s = tiles("w1_lo_s", PACK, [P, 2 * P], U8)
-        w1_hi_w = tiles("w1_hi_w", 2, [P, PASS], U32)
-        w1_hi_s = tiles("w1_hi_s", 2, [P, PASS], U8)
+        stage_lo = tiles("stage_lo", LOW, [P, PASSES * PACK * P], F32)
+        stage_hi = tiles("stage_hi", PASSES, [P, PACK * PASS], F32)
+        bf_lo = tiles("bf_lo", LOW, [P, PASSES * PACK * P], BF16)
+        bf_hi = tiles("bf_hi", PASSES, [P, PACK * PASS], BF16)
+        w1_lo_w = tiles("w1_lo_w", LOW, [P, PASSES * P], U32)
+        w1_lo_s = tiles("w1_lo_s", LOW, [P, PASSES * P], U8)
+        w1_hi_w = tiles("w1_hi_w", PASSES, [P, PASS], U32)
+        w1_hi_s = tiles("w1_hi_s", PASSES, [P, PASS], U8)
         page = tiles("page", SLICES, [P, T2], F32)
-        h_sb = tiles("h_sb", 3, [P, S], F32)
-        gap = tiles("gap", 3, [P, S], F32)
-        ring = tiles("ring", 2, [P, S], F32)
+        h_sb = tiles("h_sb", RINGS, [P, S], F32)
+        gap = tiles("gap", GAPS, [P, S], F32)
+        ring = tiles("ring", RINGS, [P, S], F32)
         x_dealt = sb.tile([P, PACK * J], F32, align_bytes=64)
-        x_lo_w = sb.tile([P, J], U32, align_bytes=64)
+        x_rows = tiles("x_rows", RINGS, [P, J], F32)
         x_lo_s = sb.tile([P, J], U8, align_bytes=64)
-        x_bf = tiles("x_bf", 2, [P, PACK * max(CHUNKS)], BF16)
-        x_hi_w = tiles("x_hi_w", 2, [P, max(CHUNKS)], U32)
-        x_hi_s = tiles("x_hi_s", 2, [P, max(CHUNKS)], U8)
-        w4_w = tiles("w4_w", 2, [P, 2 * N], U8)
-        w4_s = sb.tile([P, 2 * N], U8, align_bytes=64)
+        x_bf = tiles("x_bf", RINGS, [P, PACK * max(CHUNKS)], BF16)
+        x_hi_w = tiles("x_hi_w", RINGS, [P, max(CHUNKS)], U32)
+        x_hi_s = tiles("x_hi_s", RINGS, [P, max(CHUNKS)], U8)
+        w4_w = tiles("w4_w", PASSES, [P, 2 * N], U8)
+        w4_s = sb.tile([P, PASSES * N], U8, align_bytes=64)
         lift_sb = tiles("lift_sb", SLICES, [P, 1], F32)
         lift1 = tiles("lift1", SLICES, [P, 1], F32)
-        b2_sb = sb.tile([P, N // P], F32, align_bytes=64)
-        res = [sb.tile([P, (N // P) * w], F32, name=f"res{c}", align_bytes=64) for c, w in enumerate(CHUNKS)]
-        banks = [ps.tile([P, BANK], F32, name=f"bank{i}") for i in range(8)]
-
-        scaled = stage_lo[1:] + [stage_hi[1]] + [ring[k % 2] for k in range(PACK, SLICES)]
+        b2_sb = sb.tile([P, N_TILES], F32, align_bytes=64)
+        res = [sb.tile([P, N_TILES * w], F32, name=f"res{c}", align_bytes=64) for c, w in enumerate(CHUNKS)]
+        banks = [ps.tile([P, BANK], F32, name=f"bank{i}") for i in range(BANKS)]
 
         def rows_of(dram, k):
-            if k < PACK:
+            if k < LOW:
                 return dram[k * P : (k + 1) * P, :]
-            return dram[PASS:, :].rearrange("(p t) c -> t p c", t=PACK)[k - PACK]
+            return dram[PASS:, :].rearrange("(p t) c -> t p c", t=PACK)[k - LOW]
 
-        def load_tab_words(a, pieces):
+        def h_bank(k, half):
+            return banks[(2 * k + half) % BANKS]
+
+        def load_tab_words(a, loads):
             words = tab_words[a].rearrange("p t i -> p (t i)").bitcast(I32)
-            for i in range(pieces):
-                cols = slice(i * T // pieces, (i + 1) * T // pieces)
+            for i in range(loads):
+                cols = slice(i * T // loads, (i + 1) * T // loads)
                 nc.sync.dma_start(tab_w[a][:, cols].bitcast(I32), words[:, cols])
 
-        def load_w1_lo(u):
-            for a in range(2):
+        def load_w1_lo(k):
+            for a in range(PASSES):
                 nc.sync.dma_start(
-                    stage_lo[u][:, a * PASS : (a + 1) * PASS].rearrange("p (j c) -> p j c", j=PACK),
-                    w1[a * PASS : (a + 1) * PASS, u * P : (u + 1) * P].rearrange("(p j) c -> p j c", j=PACK),
+                    stage_lo[k][:, a * PASS : (a + 1) * PASS].rearrange("p (e c) -> p e c", e=PACK),
+                    w1[a * PASS : (a + 1) * PASS, k * P : (k + 1) * P].rearrange("(p e) c -> p e c", e=PACK),
                 )
 
         def load_w1_hi():
-            for a in range(2):
+            for a in range(PASSES):
                 nc.sync.dma_start(
-                    stage_hi[a][:].rearrange("p (j c) -> p j c", j=PACK),
-                    w1[a * PASS : (a + 1) * PASS, PASS:].rearrange("(p j) c -> p j c", j=PACK),
+                    stage_hi[a][:].rearrange("p (e c) -> p e c", e=PACK),
+                    w1[a * PASS : (a + 1) * PASS, PASS:].rearrange("(p e) c -> p e c", e=PACK),
                 )
 
         def load_lift(k):
             with nc.allow_non_contiguous_dma(reason="one value of lift for each partition"):
                 nc.sync.dma_start(lift_sb[k][:], rows_of(lift.rearrange("(r o) -> r o", o=1), k))
 
-        def quantize_w1_lo(u):
-            for a in range(2):
+        def round_interleaved(copy, dst, src):
+            copy(
+                dst.rearrange("p (c i e) -> p c e i", i=RUN, e=PACK),
+                src.rearrange("p e (c i) -> p c e i", i=RUN),
+            )
+
+        def quantize_w1_lo(k):
+            for a in range(PASSES):
                 cols = slice(a * PASS, (a + 1) * PASS)
-                nc.scalar.copy(
-                    bf_lo[u][:, cols].rearrange("p (c i j) -> p c j i", i=LINE, j=PACK),
-                    stage_lo[u][:, cols].rearrange("p (j c i) -> p c j i", j=PACK, i=LINE),
+                round_interleaved(
+                    nc.scalar.copy, bf_lo[k][:, cols], stage_lo[k][:, cols].rearrange("p (e c) -> p e c", e=PACK)
                 )
-            nc.vector.quantize_mx(out=w1_lo_w[u][:].bitcast(E4M3), scales=w1_lo_s[u][:], in_=bf_lo[u][:])
+            nc.vector.quantize_mx(out=w1_lo_w[k][:].bitcast(E4M3), scales=w1_lo_s[k][:], in_=bf_lo[k][:])
 
         def quantize_w1_hi(a):
             nc.scalar.copy(
-                bf_hi[a][:].rearrange("p (t m j) -> p m t j", t=PACK, j=PACK),
-                stage_hi[a][:].rearrange("p (j m t) -> p m t j", j=PACK, t=PACK),
+                bf_hi[a][:].rearrange("p (t m e) -> p m t e", t=PACK, e=PACK),
+                stage_hi[a][:].rearrange("p (e m t) -> p m t e", e=PACK, t=PACK),
             )
             nc.vector.quantize_mx(out=w1_hi_w[a][:].bitcast(E4M3), scales=w1_hi_s[a][:], in_=bf_hi[a][:])
 
-        def first_product(k, half):
-            js = slice(half * BANK, (half + 1) * BANK)
-            for a in range(2):
-                if k < PACK:
-                    w_words, w_scales, cols = w1_lo_w[k], w1_lo_s[k], slice(a * P, (a + 1) * P)
-                else:
-                    w_words, w_scales, cols = w1_hi_w[a], w1_hi_s[a], slice((k - PACK) * P, (k - PACK + 1) * P)
-                v_words = v_w0[:, js] if a == 0 else v_w1[half][:]
-                nc.tensor.matmul_mx(
-                    out=banks[(2 * k + half) % 8][:],
-                    lhsT=w_words[:, cols].bitcast(E4M3),
-                    lhsT_scale=w_scales[:, cols],
-                    rhs=v_words.bitcast(E4M3),
-                    rhs_scale=v_s[PACK * a : P, js],
-                    start=(a == 0),
-                    stop=(a == 1),
-                )
-
         def make_h(k):
-            for half in range(2):
-                first_product(k, half)
-                nc.scalar.copy(h_sb[k % 3][:, half * BANK : (half + 1) * BANK], banks[(2 * k + half) % 8][:])
+            for half in range(S // BANK):
+                js = slice(half * BANK, (half + 1) * BANK)
+                for a in range(PASSES):
+                    if k < LOW:
+                        w_words, w_scales, cols = w1_lo_w[k], w1_lo_s[k], slice(a * P, (a + 1) * P)
+                    else:
+                        w_words, w_scales, cols = w1_hi_w[a], w1_hi_s[a], slice((k - LOW) * P, (k - LOW + 1) * P)
+                    v_words = v_w0[:, js] if a == 0 else v_w1[half][:]
+                    nc.tensor.matmul_mx(
+                        out=h_bank(k, half)[:],
+                        lhsT=w_words[:, cols].bitcast(E4M3),
+                        lhsT_scale=w_scales[:, cols],
+                        rhs=v_words.bitcast(E4M3),
+                        rhs_scale=v_s[SCALE_ROWS * a : P, js],
+                        start=(a == 0),
+                        stop=(a == PASSES - 1),
+                    )
+                nc.scalar.copy(h_sb[k % RINGS][:, js], h_bank(k, half)[:])
 
-        def fetch_old(k, pieces):
-            w = S // pieces
-            for i in range(pieces):
-                js = slice(i * w, (i + 1) * w)
-                nc.vector.tensor_tensor(
-                    gap[k % 3][:, js],
-                    page[k][:].indirect(idx2[:, i * w // GROUP : (i + 1) * w // GROUP]),
-                    h_sb[k % 3][:, js],
-                    ALU.subtract,
-                )
+        def entries(lst, js):
+            return lst[:, js.start // GROUP : js.stop // GROUP]
+
+        def fetch_old(k, js):
+            nc.vector.tensor_tensor(
+                gap[k % GAPS][:, js], page[k][:].indirect(entries(idx2, js)), h_sb[k % RINGS][:, js], ALU.subtract
+            )
+
+        def make_lift1(k):
+            nc.scalar.activation(lift1[k][:], lift_sb[k][:], ACT.Copy, bias=1.0)
 
         def scale_h(k, half, dst):
-            nc.scalar.activation(dst, banks[(2 * k + half) % 8][:], ACT.Copy, scale=lift1[k][:])
+            nc.scalar.activation(dst, h_bank(k, half)[:], ACT.Copy, scale=lift1[k][:])
 
-        def scatter(k, js, addend):
-            nc.scalar.activation(gap[k % 3][:, js], gap[k % 3][:, js], ACT.Relu)
-            offsets = idx2[:, js.start // GROUP : js.stop // GROUP]
-            nc.vector.tensor_tensor(page[k][:].indirect(offsets), gap[k % 3][:, js], addend, ALU.add)
+        def put_new(k, js, scaled_h):
+            nc.scalar.activation(gap[k % GAPS][:, js], gap[k % GAPS][:, js], ACT.Relu)
+            nc.vector.tensor_tensor(page[k][:].indirect(entries(idx2, js)), gap[k % GAPS][:, js], scaled_h, ALU.add)
 
-        def put_new(k):
-            nc.scalar.activation(lift1[k][:], lift_sb[k][:], ACT.Copy, bias=1.0)
-            for half in range(2):
-                scale_h(k, half, scaled[k][:, half * BANK : (half + 1) * BANK])
-            scatter(k, slice(0, S), scaled[k][:, :S])
+        def fetch_slice(k):
+            nc.sync.dma_start(page[k][:], rows_of(page0, k))
+            make_h(k)
+            fetch_old(k, slice(0, S))
 
-        def fetch_x_lo(u):
-            nc.vector.tensor_tensor(h_sb[(u + 1) % 3][:], page[u][:].indirect(idx3[:]), stage_lo[u][:], ALU.add)
+        def update_slice(k):
+            make_lift1(k)
+            for half in range(S // BANK):
+                scale_h(k, half, ring[k % RINGS][:, half * BANK : (half + 1) * BANK])
+            put_new(k, slice(0, S), ring[k % RINGS][:])
 
-        def deal_x_lo(u):
-            nc.scalar.dma_start(x_dealt[QUAD * u : QUAD * (u + 1), :], h_sb[(u + 1) % 3][:])
-
-        def round_x(copy, dst, src):
-            copy(
-                dst.rearrange("p (c i t) -> p c t i", i=LINE, t=PACK),
-                src.rearrange("p t (c i) -> p c t i", i=LINE),
-            )
+        def fetch_x_lo(k):
+            nc.sync.dma_start(stage_lo[k][:], rows_of(base, k))
+            nc.vector.tensor_tensor(x_rows[k % RINGS][:], page[k][:].indirect(idx3[:]), stage_lo[k][:], ALU.add)
+            nc.gpsimd.dma_start(x_dealt[QUAD * k : QUAD * (k + 1), :], x_rows[k % RINGS][:])
 
         nc.gpsimd.memset(tab_s[:].bitcast(I32), 0)
         nc.vector.memset(w4_s[:].bitcast(I32), 0)
         nc.sync.dma_start(idx[:], offs)
-        load_tab_words(0, 4)
+        load_tab_words(0, FIRST_LOADS)
         nc.sync.dma_start(idx2[:], offs2)
         load_w1_lo(0)
         for q in range(P // QUAD):
             nc.sync.dma_start(
-                tab_s[QUAD * q : QUAD * q + 2 * PACK, :].bitcast(I32),
-                tab_scales[:, PACK * q : PACK * (q + 1), :].bitcast(I32),
+                tab_s[QUAD * q : QUAD * q + PASSES * SCALE_ROWS, :].bitcast(I32),
+                tab_scales[:, SCALE_ROWS * q : SCALE_ROWS * (q + 1), :].bitcast(I32),
             )
         load_tab_words(1, 1)
         nc.sync.dma_start(page[0][:], rows_of(page0, 0))
         load_lift(0)
 
+        halves = (slice(0, BANK), slice(BANK, S))
         nc.vector.tensor_copy(v_w0[:], tab_w[0][:].indirect(idx[:]))
         nc.vector.tensor_copy(v_s[:], tab_s[:].indirect(idx[:]))
         quantize_w1_lo(0)
-        for half in range(2):
-            cols = slice(half * BANK // GROUP, (half + 1) * BANK // GROUP)
-            nc.vector.tensor_copy(v_w1[half][:], tab_w[1][:].indirect(idx[:, cols]))
+        for half, js in enumerate(halves):
+            nc.vector.tensor_copy(v_w1[half][:], tab_w[1][:].indirect(entries(idx, js)))
+
         make_h(0)
-        fetch_old(0, 2)
-        nc.scalar.activation(lift1[0][:], lift_sb[0][:], ACT.Copy, bias=1.0)
+        for js in halves:
+            fetch_old(0, js)
+        make_lift1(0)
         scale_h(0, 0, ring[0][:, :BANK])
-        scatter(0, slice(0, BANK), ring[0][:, :BANK])
-        load_w1_lo(1)
-        quantize_w1_lo(1)
-        scale_h(0, 1, stage_lo[1][:, :BANK])
-        scatter(0, slice(BANK, S), stage_lo[1][:, :BANK])
+        put_new(0, halves[0], ring[0][:, :BANK])
+        for k in (1, 2):
+            load_w1_lo(k)
+            quantize_w1_lo(k)
+        scale_h(0, 1, stage_lo[2][:, :BANK])
+        put_new(0, halves[1], stage_lo[2][:, :BANK])
 
+        fetch_slice(1)
         nc.sync.dma_start(idx3[:], offs3)
-
-        def fetch_slice(k):
-            nc.sync.dma_start(page[k][:], rows_of(page0, k))
-            make_h(k)
-            fetch_old(k, 1)
-
         for k in range(1, SLICES):
-            if k < PACK:
-                load_lift(k)
-            if k + 1 < PACK:
-                load_w1_lo(k + 1)
-            if k + 1 == PACK:
+            if k + 2 < LOW:
+                load_w1_lo(k + 2)
+                quantize_w1_lo(k + 2)
+            if k + 2 == LOW:
                 load_w1_hi()
-            if k <= PACK:
-                nc.sync.dma_start(stage_lo[k - 1][:], rows_of(base, k - 1))
-                fetch_slice(k)
-                fetch_x_lo(k - 1)
-            if k + 1 < PACK:
-                quantize_w1_lo(k + 1)
-            if k + 1 == PACK:
-                for a in range(2):
+                for a in range(PASSES):
                     quantize_w1_hi(a)
-            if PACK <= k < SLICES - 1:
+            if k + 1 < SLICES:
                 fetch_slice(k + 1)
-            if k >= PACK:
-                load_lift(k)
-            put_new(k)
-            if k <= PACK:
-                deal_x_lo(k - 1)
+            load_lift(k)
+            update_slice(k)
+            if k <= LOW:
+                fetch_x_lo(k - 1)
 
-        for half in range(2):
+        for half, js in enumerate(halves):
             nc.sync.dma_start(
                 stage_hi[half][:].rearrange("p (t j) -> p t j", t=PACK),
-                base[PASS:, half * BANK : (half + 1) * BANK].rearrange("(p t) j -> p t j", t=PACK),
+                base[PASS:, js].rearrange("(p t) j -> p t j", t=PACK),
             )
-        for a in range(2):
-            nc.sync.dma_start(w4_w[a][:].bitcast(I32), w4_words[a].bitcast(I32))
+        for b in range(PASSES):
+            nc.sync.dma_start(w4_w[b][:].bitcast(I32), w4_words[b].bitcast(I32))
         for q in range(P // QUAD):
             nc.sync.dma_start(
-                w4_s[QUAD * q : QUAD * q + PACK, :].bitcast(I32).rearrange("r (a c) -> r a c", a=2),
-                w4_scales[:, PACK * q : PACK * (q + 1), :].bitcast(I32).rearrange("a r c -> r a c"),
+                w4_s[QUAD * q : QUAD * q + SCALE_ROWS, :].bitcast(I32).rearrange("s (b c) -> s b c", b=PASSES),
+                w4_scales[:, SCALE_ROWS * q : SCALE_ROWS * (q + 1), :].bitcast(I32).rearrange("b s c -> s b c"),
             )
         with nc.allow_non_contiguous_dma(reason="one bias value for each partition and tile of n"):
             nc.sync.dma_start(b2_sb[:], b2.rearrange("(u p) -> p u", p=P))
 
+        last = SLICES - 1
         x_lo_bf = [
             sb.tile([P, 2 * PACK * PIECE], BF16, name=f"x_lo_bf{i}", tag=tag, align_bytes=64)
-            for i, tag in enumerate((f"h_sb{(SLICES - 1) % 3}", f"ring{(SLICES - 2) % 2}"))
+            for i, tag in enumerate((f"h_sb{last % RINGS}", f"ring{(last - 1) % RINGS}"))
         ]
         x_lo_pieces = [
             x_lo_bf[i // 2][:, (i % 2) * PACK * PIECE : (i % 2 + 1) * PACK * PIECE] for i in range(J // PIECE)
         ]
         for i in range(J // PIECE):
-            round_x(
+            round_interleaved(
                 nc.scalar.copy,
                 x_lo_pieces[i],
                 x_dealt[:].rearrange("p (t j) -> p t j", t=PACK)[:, :, i * PIECE : (i + 1) * PIECE],
             )
 
-        x_hi = (ring[(SLICES - 1) % 2], gap[(SLICES - 1) % 3])
+        x_lo_w = sb.tile([P, J], U32, tag=f"gap{(last - 2) % GAPS}", align_bytes=64)
+        x_hi = (ring[last % RINGS], gap[last % GAPS])
         starts = [sum(CHUNKS[:c]) for c in range(len(CHUNKS))]
 
         def fetch_x_hi(c):
@@ -278,51 +277,48 @@ def tile_list_substation_page_features_kernel(
             half, off = divmod(j0, BANK)
             for t in range(PACK):
                 nc.vector.tensor_tensor(
-                    x_hi[c % 2][:, t * w : (t + 1) * w],
-                    page[PACK + t][:].indirect(idx3[:, j0 // GROUP : (j0 + w) // GROUP]),
+                    x_hi[c % RINGS][:, t * w : (t + 1) * w],
+                    page[LOW + t][:].indirect(entries(idx3, slice(j0, j0 + w))),
                     stage_hi[half][:, t * BANK + off : t * BANK + off + w],
                     ALU.add,
                 )
             if j0 % PIECE == 0:
                 js = slice(j0, j0 + PIECE)
-                nc.vector.quantize_mx(out=x_lo_w[:, js].bitcast(E4M3), scales=x_lo_s[:, js], in_=x_lo_pieces[j0 // PIECE])
-            round_x(
+                nc.vector.quantize_mx(
+                    out=x_lo_w[:, js].bitcast(E4M3), scales=x_lo_s[:, js], in_=x_lo_pieces[j0 // PIECE]
+                )
+            round_interleaved(
                 nc.vector.tensor_copy if c >= len(CHUNKS) - VECTOR_ROUNDS else nc.scalar.copy,
-                x_bf[c % 2][:, : PACK * w],
-                x_hi[c % 2][:, : PACK * w].rearrange("p (t j) -> p t j", t=PACK),
+                x_bf[c % RINGS][:, : PACK * w],
+                x_hi[c % RINGS][:, : PACK * w].rearrange("p (t j) -> p t j", t=PACK),
             )
 
         def second_product(c):
             j0, w = starts[c], CHUNKS[c]
-            nc.vector.quantize_mx(
-                out=x_hi_w[c % 2][:, :w].bitcast(E4M3), scales=x_hi_s[c % 2][:, :w], in_=x_bf[c % 2][:, : PACK * w]
-            )
-            operands = (
-                (x_lo_w[:, j0 : j0 + w], x_lo_s[:, j0 : j0 + w]),
-                (x_hi_w[c % 2][:, :w], x_hi_s[c % 2][:, :w]),
-            )
+            hi_words, hi_scales = x_hi_w[c % RINGS][:, :w], x_hi_s[c % RINGS][:, :w]
+            nc.vector.quantize_mx(out=hi_words.bitcast(E4M3), scales=hi_scales, in_=x_bf[c % RINGS][:, : PACK * w])
+            sums = [banks[(N_TILES * c + u) % BANKS][:, :w] for u in range(N_TILES)]
+            operands = ((x_lo_w[:, j0 : j0 + w], x_lo_s[:, j0 : j0 + w]), (hi_words, hi_scales))
             for b, (x_words, x_scales) in enumerate(operands):
-                for u in range(N // P):
+                for u in range(N_TILES):
                     nc.tensor.matmul_mx(
-                        out=banks[(PACK * c + u) % 8][:, :w],
+                        out=sums[u],
                         lhsT=w4_w[b][:, 2 * u * P : 2 * (u + 1) * P].bitcast(E2M1),
                         lhsT_scale=w4_s[:, b * N + u * P : b * N + (u + 1) * P],
                         rhs=x_words.bitcast(E4M3),
                         rhs_scale=x_scales,
                         start=(b == 0),
-                        stop=(b == 1),
+                        stop=(b == PASSES - 1),
                     )
-            for u in range(N // P):
-                nc.scalar.activation(
-                    res[c][:, u * w : (u + 1) * w], banks[(PACK * c + u) % 8][:, :w], ACT.Abs, bias=b2_sb[:, u : u + 1]
-                )
+            for u in range(N_TILES):
+                nc.scalar.activation(res[c][:, u * w : (u + 1) * w], sums[u], ACT.Abs, bias=b2_sb[:, u : u + 1])
             dst = out[:, j0 : j0 + w].rearrange("(u p) j -> p u j", p=P)
             src = res[c][:].rearrange("p (u j) -> p u j", j=w)
             if c + 1 < len(CHUNKS):
                 nc.sync.dma_start(dst, src)
             else:
-                nc.sync.dma_start(dst[:, :2], src[:, :2])
-                nc.scalar.dma_start(dst[:, 2:], src[:, 2:])
+                nc.sync.dma_start(dst[:, : N_TILES // 2], src[:, : N_TILES // 2])
+                nc.scalar.dma_start(dst[:, N_TILES // 2 :], src[:, N_TILES // 2 :])
 
         for c in range(len(CHUNKS) + 1):
             if c < len(CHUNKS):

from contextlib import ExitStack

import concourse.mybir as mybir

K, T, S, H, T2, J, N = 1024, 2048, 1024, 1024, 2048, 1024, 512
FLOPS = 2 * K * H * S + 2 * H * N * J

F32 = mybir.dt.float32
BF16 = mybir.dt.bfloat16
I32 = mybir.dt.int32
U32 = mybir.dt.uint32
U16 = mybir.dt.uint16
U8 = mybir.dt.uint8
E4M3 = mybir.dt.float8_e4m3fn_x4
E2M1 = mybir.dt.float4_e2m1fn_x4
ACT = mybir.ActivationFunctionType
ALU = mybir.AluOpType

P = 128
PACK = 4
PASS = P * PACK
PASSES = 2
QUAD = 32
SCALE_ROWS = 4
BANK = 512
BANKS = 8
GROUP = 16
RUN = 4
SLICES = H // P
LOW = PASS // P
N_TILES = N // P
PIECE = 256
CHUNKS = (256, 256, 256, 128, 128)
VECTOR_ROUNDS = 2
FIRST_LOADS = 4
GAPS = 3
RINGS = 2


def tile_list_substation_page_features_kernel(
    tc, tab_words, tab_scales, w1, w4_words, w4_scales, lift, page0, base, b2, offs, offs2, offs3, out
):
    nc = tc.nc
    with ExitStack() as ctx:
        sb = ctx.enter_context(tc.tile_pool(name="sb", bufs=1))
        ps = ctx.enter_context(tc.psum_pool(name="ps", bufs=1))

        def tiles(name, count, shape, dtype):
            return [sb.tile(shape, dtype, name=f"{name}{i}", align_bytes=64) for i in range(count)]

        idx, idx2, idx3 = tiles("idx", 3, [P, S // GROUP], U16)
        tab_w = tiles("tab_w", PASSES, [P, T], U32)
        tab_s = sb.tile([P, T], U8, align_bytes=64)
        v_w0 = sb.tile([P, S], U32, align_bytes=64)
        v_w1 = tiles("v_w1", S // BANK, [P, BANK], U32)
        v_s = sb.tile([P, S], U8, align_bytes=64)
        stage_lo = tiles("stage_lo", LOW, [P, PASSES * PACK * P], F32)
        stage_hi = tiles("stage_hi", PASSES, [P, PACK * PASS], F32)
        bf_lo = tiles("bf_lo", LOW, [P, PASSES * PACK * P], BF16)
        bf_hi = tiles("bf_hi", PASSES, [P, PACK * PASS], BF16)
        w1_lo_w = tiles("w1_lo_w", LOW, [P, PASSES * P], U32)
        w1_lo_s = tiles("w1_lo_s", LOW, [P, PASSES * P], U8)
        w1_hi_w = tiles("w1_hi_w", PASSES, [P, PASS], U32)
        w1_hi_s = tiles("w1_hi_s", PASSES, [P, PASS], U8)
        page = tiles("page", SLICES, [P, T2], F32)
        h_sb = tiles("h_sb", RINGS, [P, S], F32)
        gap = tiles("gap", GAPS, [P, S], F32)
        ring = tiles("ring", RINGS, [P, S], F32)
        x_dealt = sb.tile([P, PACK * J], F32, align_bytes=64)
        x_rows = tiles("x_rows", RINGS, [P, J], F32)
        x_lo_s = sb.tile([P, J], U8, align_bytes=64)
        x_bf = tiles("x_bf", RINGS, [P, PACK * max(CHUNKS)], BF16)
        x_hi_w = tiles("x_hi_w", RINGS, [P, max(CHUNKS)], U32)
        x_hi_s = tiles("x_hi_s", RINGS, [P, max(CHUNKS)], U8)
        w4_w = tiles("w4_w", PASSES, [P, 2 * N], U8)
        w4_s = sb.tile([P, PASSES * N], U8, align_bytes=64)
        lift_sb = tiles("lift_sb", SLICES, [P, 1], F32)
        lift1 = tiles("lift1", SLICES, [P, 1], F32)
        b2_sb = sb.tile([P, N_TILES], F32, align_bytes=64)
        res = [sb.tile([P, N_TILES * w], F32, name=f"res{c}", align_bytes=64) for c, w in enumerate(CHUNKS)]
        banks = [ps.tile([P, BANK], F32, name=f"bank{i}") for i in range(BANKS)]

        def rows_of(dram, k):
            if k < LOW:
                return dram[k * P : (k + 1) * P, :]
            return dram[PASS:, :].rearrange("(p t) c -> t p c", t=PACK)[k - LOW]

        def h_bank(k, half):
            return banks[(2 * k + half) % BANKS]

        def load_tab_words(a, loads):
            words = tab_words[a].rearrange("p t i -> p (t i)").bitcast(I32)
            for i in range(loads):
                cols = slice(i * T // loads, (i + 1) * T // loads)
                nc.sync.dma_start(tab_w[a][:, cols].bitcast(I32), words[:, cols])

        def load_w1_lo(k):
            for a in range(PASSES):
                nc.sync.dma_start(
                    stage_lo[k][:, a * PASS : (a + 1) * PASS].rearrange("p (e c) -> p e c", e=PACK),
                    w1[a * PASS : (a + 1) * PASS, k * P : (k + 1) * P].rearrange("(p e) c -> p e c", e=PACK),
                )

        def load_w1_hi():
            for a in range(PASSES):
                nc.sync.dma_start(
                    stage_hi[a][:].rearrange("p (e c) -> p e c", e=PACK),
                    w1[a * PASS : (a + 1) * PASS, PASS:].rearrange("(p e) c -> p e c", e=PACK),
                )

        def load_lift(k):
            with nc.allow_non_contiguous_dma(reason="one value of lift for each partition"):
                nc.sync.dma_start(lift_sb[k][:], rows_of(lift.rearrange("(r o) -> r o", o=1), k))

        def round_interleaved(copy, dst, src):
            copy(
                dst.rearrange("p (c i e) -> p c e i", i=RUN, e=PACK),
                src.rearrange("p e (c i) -> p c e i", i=RUN),
            )

        def quantize_w1_lo(k):
            for a in range(PASSES):
                cols = slice(a * PASS, (a + 1) * PASS)
                round_interleaved(
                    nc.scalar.copy, bf_lo[k][:, cols], stage_lo[k][:, cols].rearrange("p (e c) -> p e c", e=PACK)
                )
            nc.vector.quantize_mx(out=w1_lo_w[k][:].bitcast(E4M3), scales=w1_lo_s[k][:], in_=bf_lo[k][:])

        def quantize_w1_hi(a):
            nc.scalar.copy(
                bf_hi[a][:].rearrange("p (t m e) -> p m t e", t=PACK, e=PACK),
                stage_hi[a][:].rearrange("p (e m t) -> p m t e", e=PACK, t=PACK),
            )
            nc.vector.quantize_mx(out=w1_hi_w[a][:].bitcast(E4M3), scales=w1_hi_s[a][:], in_=bf_hi[a][:])

        def make_h(k):
            for half in range(S // BANK):
                js = slice(half * BANK, (half + 1) * BANK)
                for a in range(PASSES):
                    if k < LOW:
                        w_words, w_scales, cols = w1_lo_w[k], w1_lo_s[k], slice(a * P, (a + 1) * P)
                    else:
                        w_words, w_scales, cols = w1_hi_w[a], w1_hi_s[a], slice((k - LOW) * P, (k - LOW + 1) * P)
                    v_words = v_w0[:, js] if a == 0 else v_w1[half][:]
                    nc.tensor.matmul_mx(
                        out=h_bank(k, half)[:],
                        lhsT=w_words[:, cols].bitcast(E4M3),
                        lhsT_scale=w_scales[:, cols],
                        rhs=v_words.bitcast(E4M3),
                        rhs_scale=v_s[SCALE_ROWS * a : P, js],
                        start=(a == 0),
                        stop=(a == PASSES - 1),
                    )
                nc.scalar.copy(h_sb[k % RINGS][:, js], h_bank(k, half)[:])

        def entries(lst, js):
            return lst[:, js.start // GROUP : js.stop // GROUP]

        def fetch_old(k, js):
            nc.vector.tensor_tensor(
                gap[k % GAPS][:, js], page[k][:].indirect(entries(idx2, js)), h_sb[k % RINGS][:, js], ALU.subtract
            )

        def make_lift1(k):
            nc.scalar.activation(lift1[k][:], lift_sb[k][:], ACT.Copy, bias=1.0)

        def scale_h(k, half, dst):
            nc.scalar.activation(dst, h_bank(k, half)[:], ACT.Copy, scale=lift1[k][:])

        def put_new(k, js, scaled_h):
            nc.scalar.activation(gap[k % GAPS][:, js], gap[k % GAPS][:, js], ACT.Relu)
            nc.vector.tensor_tensor(page[k][:].indirect(entries(idx2, js)), gap[k % GAPS][:, js], scaled_h, ALU.add)

        def fetch_slice(k):
            nc.sync.dma_start(page[k][:], rows_of(page0, k))
            make_h(k)
            fetch_old(k, slice(0, S))

        def update_slice(k):
            make_lift1(k)
            for half in range(S // BANK):
                scale_h(k, half, ring[k % RINGS][:, half * BANK : (half + 1) * BANK])
            put_new(k, slice(0, S), ring[k % RINGS][:])

        def fetch_x_lo(k):
            nc.sync.dma_start(stage_lo[k][:], rows_of(base, k))
            nc.vector.tensor_tensor(x_rows[k % RINGS][:], page[k][:].indirect(idx3[:]), stage_lo[k][:], ALU.add)
            nc.gpsimd.dma_start(x_dealt[QUAD * k : QUAD * (k + 1), :], x_rows[k % RINGS][:])

        nc.gpsimd.memset(tab_s[:].bitcast(I32), 0)
        nc.vector.memset(w4_s[:].bitcast(I32), 0)
        nc.sync.dma_start(idx[:], offs)
        load_tab_words(0, FIRST_LOADS)
        nc.sync.dma_start(idx2[:], offs2)
        load_w1_lo(0)
        for q in range(P // QUAD):
            nc.sync.dma_start(
                tab_s[QUAD * q : QUAD * q + PASSES * SCALE_ROWS, :].bitcast(I32),
                tab_scales[:, SCALE_ROWS * q : SCALE_ROWS * (q + 1), :].bitcast(I32),
            )
        load_tab_words(1, 1)
        nc.sync.dma_start(page[0][:], rows_of(page0, 0))
        load_lift(0)

        halves = (slice(0, BANK), slice(BANK, S))
        nc.vector.tensor_copy(v_w0[:], tab_w[0][:].indirect(idx[:]))
        nc.vector.tensor_copy(v_s[:], tab_s[:].indirect(idx[:]))
        quantize_w1_lo(0)
        for half, js in enumerate(halves):
            nc.vector.tensor_copy(v_w1[half][:], tab_w[1][:].indirect(entries(idx, js)))

        make_h(0)
        for js in halves:
            fetch_old(0, js)
        make_lift1(0)
        scale_h(0, 0, ring[0][:, :BANK])
        put_new(0, halves[0], ring[0][:, :BANK])
        for k in (1, 2):
            load_w1_lo(k)
            quantize_w1_lo(k)
        scale_h(0, 1, stage_lo[2][:, :BANK])
        put_new(0, halves[1], stage_lo[2][:, :BANK])

        fetch_slice(1)
        nc.sync.dma_start(idx3[:], offs3)
        for k in range(1, SLICES):
            if k + 2 < LOW:
                load_w1_lo(k + 2)
                quantize_w1_lo(k + 2)
            if k + 2 == LOW:
                load_w1_hi()
                for a in range(PASSES):
                    quantize_w1_hi(a)
            if k + 1 < SLICES:
                fetch_slice(k + 1)
            load_lift(k)
            update_slice(k)
            if k <= LOW:
                fetch_x_lo(k - 1)

        for half, js in enumerate(halves):
            nc.sync.dma_start(
                stage_hi[half][:].rearrange("p (t j) -> p t j", t=PACK),
                base[PASS:, js].rearrange("(p t) j -> p t j", t=PACK),
            )
        for b in range(PASSES):
            nc.sync.dma_start(w4_w[b][:].bitcast(I32), w4_words[b].bitcast(I32))
        for q in range(P // QUAD):
            nc.sync.dma_start(
                w4_s[QUAD * q : QUAD * q + SCALE_ROWS, :].bitcast(I32).rearrange("s (b c) -> s b c", b=PASSES),
                w4_scales[:, SCALE_ROWS * q : SCALE_ROWS * (q + 1), :].bitcast(I32).rearrange("b s c -> s b c"),
            )
        with nc.allow_non_contiguous_dma(reason="one bias value for each partition and tile of n"):
            nc.sync.dma_start(b2_sb[:], b2.rearrange("(u p) -> p u", p=P))

        last = SLICES - 1
        x_lo_bf = [
            sb.tile([P, 2 * PACK * PIECE], BF16, name=f"x_lo_bf{i}", tag=tag, align_bytes=64)
            for i, tag in enumerate((f"h_sb{last % RINGS}", f"ring{(last - 1) % RINGS}"))
        ]
        x_lo_pieces = [
            x_lo_bf[i // 2][:, (i % 2) * PACK * PIECE : (i % 2 + 1) * PACK * PIECE] for i in range(J // PIECE)
        ]
        for i in range(J // PIECE):
            round_interleaved(
                nc.scalar.copy,
                x_lo_pieces[i],
                x_dealt[:].rearrange("p (t j) -> p t j", t=PACK)[:, :, i * PIECE : (i + 1) * PIECE],
            )

        x_lo_w = sb.tile([P, J], U32, tag=f"gap{(last - 2) % GAPS}", align_bytes=64)
        x_hi = (ring[last % RINGS], gap[last % GAPS])
        starts = [sum(CHUNKS[:c]) for c in range(len(CHUNKS))]

        def fetch_x_hi(c):
            j0, w = starts[c], CHUNKS[c]
            half, off = divmod(j0, BANK)
            for t in range(PACK):
                nc.vector.tensor_tensor(
                    x_hi[c % RINGS][:, t * w : (t + 1) * w],
                    page[LOW + t][:].indirect(entries(idx3, slice(j0, j0 + w))),
                    stage_hi[half][:, t * BANK + off : t * BANK + off + w],
                    ALU.add,
                )
            if j0 % PIECE == 0:
                js = slice(j0, j0 + PIECE)
                nc.vector.quantize_mx(
                    out=x_lo_w[:, js].bitcast(E4M3), scales=x_lo_s[:, js], in_=x_lo_pieces[j0 // PIECE]
                )
            round_interleaved(
                nc.vector.tensor_copy if c >= len(CHUNKS) - VECTOR_ROUNDS else nc.scalar.copy,
                x_bf[c % RINGS][:, : PACK * w],
                x_hi[c % RINGS][:, : PACK * w].rearrange("p (t j) -> p t j", t=PACK),
            )

        def second_product(c):
            j0, w = starts[c], CHUNKS[c]
            hi_words, hi_scales = x_hi_w[c % RINGS][:, :w], x_hi_s[c % RINGS][:, :w]
            nc.vector.quantize_mx(out=hi_words.bitcast(E4M3), scales=hi_scales, in_=x_bf[c % RINGS][:, : PACK * w])
            sums = [banks[(N_TILES * c + u) % BANKS][:, :w] for u in range(N_TILES)]
            operands = ((x_lo_w[:, j0 : j0 + w], x_lo_s[:, j0 : j0 + w]), (hi_words, hi_scales))
            for b, (x_words, x_scales) in enumerate(operands):
                for u in range(N_TILES):
                    nc.tensor.matmul_mx(
                        out=sums[u],
                        lhsT=w4_w[b][:, 2 * u * P : 2 * (u + 1) * P].bitcast(E2M1),
                        lhsT_scale=w4_s[:, b * N + u * P : b * N + (u + 1) * P],
                        rhs=x_words.bitcast(E4M3),
                        rhs_scale=x_scales,
                        start=(b == 0),
                        stop=(b == PASSES - 1),
                    )
            for u in range(N_TILES):
                nc.scalar.activation(res[c][:, u * w : (u + 1) * w], sums[u], ACT.Abs, bias=b2_sb[:, u : u + 1])
            dst = out[:, j0 : j0 + w].rearrange("(u p) j -> p u j", p=P)
            src = res[c][:].rearrange("p (u j) -> p u j", j=w)
            if c + 1 < len(CHUNKS):
                nc.sync.dma_start(dst, src)
            else:
                nc.sync.dma_start(dst[:, : N_TILES // 2], src[:, : N_TILES // 2])
                nc.scalar.dma_start(dst[:, N_TILES // 2 :], src[:, N_TILES // 2 :])

        for c in range(len(CHUNKS) + 1):
            if c < len(CHUNKS):
                fetch_x_hi(c)
            if c > 0:
                second_product(c - 1)
